import numpy as np
import ml_dtypes


def mxq(x, axis, fmt="e4m3"):
    dtype, down = {"e4m3": (ml_dtypes.float8_e4m3fn, 7), "e5m2": (ml_dtypes.float8_e5m2, 14)}[fmt]
    v = np.moveaxis(np.asarray(x, np.float32).astype(ml_dtypes.bfloat16).astype(np.float64), axis, -1)
    blocks = v.reshape(v.shape[:-1] + (-1, 32))
    amax = np.abs(blocks).max(-1, keepdims=True)
    byte = np.maximum(np.where(amax > 0, np.frexp(amax)[1] - 1 + 127, 0) - down, 1)
    scale = np.exp2(byte - 127.0)
    codes = (blocks / scale).astype(np.float32).astype(dtype).astype(np.float64)
    return np.moveaxis((codes * scale).reshape(v.shape), -1, axis)


WIDE = False


def mx_kscale(k):
    if not WIDE:
        return np.ones(k)
    levels = np.array([10, -10, 5, -5, 0])
    if k % 512:
        return np.exp2(np.random.permutation(np.resize(levels, k // 32))).repeat(32)
    a = np.empty((k // 512, 16))
    for p in range(k // 512):
        a[p, :8] = np.random.permutation(np.resize(levels, 8))
        for g in range(8):
            far = levels[np.abs(levels - a[p, g]) >= 10]
            a[p, g + 8] = far[np.random.randint(len(far))]
    return np.exp2(a.ravel()).repeat(32)


def f64(x):
    return np.asarray(x).astype(np.float64)


def striped(idx):
    return np.tile(idx.reshape(-1, 16).T, (8, 1)).astype(np.uint16)


def unstriped(offs):
    return offs[:16].T.reshape(-1).astype(np.int64)


def relu(v):
    return np.maximum(v, 0.0)

def planes(y):
    n, m = y.shape
    v = y.astype(np.float32).astype(ml_dtypes.bfloat16).astype(np.float64).reshape(n // 32, 32, m)
    top = np.abs(v).max(1)
    byte = np.clip(np.where(top > 0, np.frexp(top)[1] - 1 + 127 - 7, 1), 1, 254)
    codes = (v * np.exp2(127.0 - byte)[:, None, :]).reshape(n, m).astype(np.float32).astype(ml_dtypes.float8_e4m3fn).view(np.uint8)
    words = codes.reshape(n // 512, 128, 4, m).transpose(0, 1, 3, 2)
    return np.ascontiguousarray(words), np.ascontiguousarray(byte.astype(np.uint8).reshape(n // 512, 16, m))


K, T, S, V, H = 512, 1024, 512, 256, 512


def setup_inputs():
    n = np.random.standard_normal
    s = mx_kscale(K)[:, None]
    u = mx_kscale(H)
    return {
        "xT": (n((K, T)) * s).astype(np.float32),
        "w1": (n((K, H)) / np.sqrt(K) / s * u).astype(np.float32),
        "w2": (n((H, H)) / np.sqrt(2 * H) / u[:, None]).astype(np.float32),
        "w3": (n((H, H)) / np.sqrt(2 * H) / u[:, None]).astype(np.float32),
        "offs": striped(np.random.permutation(T)[:S]),
    }


def reference(xT, w1, w2, w3, offs):
    xq = mxq(f64(xT)[:, unstriped(offs)], 0, "e4m3")
    h = relu(mxq(f64(w1), 0, "e4m3").T @ xq)
    low = 0.5 * (h[:, :V] + h[:, V:2 * V])
    high = 0.5 * (h[:, :V] - h[:, V:2 * V])
    out_0 = mxq(f64(w2), 0, "e4m3").T @ mxq(low, 0, "e4m3") + mxq(f64(w3), 0, "e4m3").T @ mxq(high, 0, "e4m3")
    return (out_0,) + planes(out_0)

@@ -1,0 +1,203 @@
+from contextlib import ExitStack
+
+import concourse.mybir as mybir
+
+F32 = mybir.dt.float32
+BF16 = mybir.dt.bfloat16
+U32 = mybir.dt.uint32
+I32 = mybir.dt.int32
+U16 = mybir.dt.uint16
+U8 = mybir.dt.uint8
+FP8X4 = mybir.dt.float8_e4m3fn_x4
+ALU = mybir.AluOpType
+ACT = mybir.ActivationFunctionType
+
+P = 128
+K, T, S, V, H = 512, 1024, 512, 256, 512
+FLOPS = 2 * K * H * S + 2 * 2 * H * H * V
+
+
+def tile_picked_haar_relu_lo_kernel(tc, xT, w1, w2, w3, offs, out_0, out_1, out_2):
+    nc = tc.nc
+    with ExitStack() as ctx:
+        keep = ctx.enter_context(tc.tile_pool(name="keep", bufs=1))
+        psum = ctx.enter_context(tc.psum_pool(name="psum", bufs=1))
+
+        def quantise(codes, scales, values):
+            nc.vector.quantize_mx(out=codes.bitcast(FP8X4), scales=scales, in_=values)
+
+        x_rows = xT.rearrange("(p j) c -> p j c", j=4)
+        offsets = keep.tile([P, S // 16], U16, name="offsets")
+        x_raw = {}
+        for u in range(2):
+            for h in range(2):
+                x_raw[u, h] = keep.tile([P, 2, 512], F32, name=f"x_raw{u}{h}")
+                nc.sync.dma_start(out=x_raw[u, h][:], in_=x_rows[:, 2 * u : 2 * u + 2, 512 * h : 512 * h + 512])
+                if (u, h) == (0, 0):
+                    nc.sync.dma_start(offsets[:], offs)
+        w_raw = {}
+        for a, w in enumerate((w1, w2, w3)):
+            w_rows = w.rearrange("(p j) c -> p j c", j=4)
+            for h in range(2):
+                w_raw[a, h] = keep.tile([P, 4, 256], F32, name=f"w_raw{a}{h}")
+                nc.sync.dma_start(out=w_raw[a, h][:], in_=w_rows[:, :, 256 * h : 256 * h + 256])
+
+        window = [keep.tile([P, T], U32, name=f"window{u}") for u in range(2)]
+
+        def cast_x(engine, u, h, c0, c1):
+            dst = window[u][:].bitcast(BF16).rearrange("p (c e) -> p c e", e=2)[:, 512 * h + c0 : 512 * h + c1, :]
+            src = x_raw[u, h][:, :, c0:c1].rearrange("p e c -> p c e")
+            if engine == "v":
+                nc.vector.tensor_copy(out=dst, in_=src)
+            else:
+                nc.scalar.activation(out=dst, in_=src, func=ACT.Copy)
+
+        w_bf = [keep.tile([P, 4, P, 4], BF16, name=f"w_bf{a}", align_bytes=64) for a in range(3)]
+        w_codes = [keep.tile([P, H], U32, name=f"w_codes{a}", align_bytes=64) for a in range(3)]
+        w_scales = [keep.tile([P, H], U8, name=f"w_scales{a}", align_bytes=64) for a in range(3)]
+
+        def cast_w(engine, a, h, m0, m1):
+            if m1 <= m0:
+                return
+            dst = w_bf[a][:, :, 64 * h + m0 : 64 * h + m1, :].rearrange("p t m j -> p m j t")
+            src = w_raw[a, h][:, :, 4 * m0 : 4 * m1].rearrange("p j (m t) -> p m j t", t=4)
+            if a == 0:
+                if engine == "v":
+                    nc.vector.tensor_scalar(out=dst, in0=src, scalar1=0.5, scalar2=None, op0=ALU.mult)
+                else:
+                    nc.scalar.activation(out=dst, in_=src, func=ACT.Copy, scale=0.5)
+            elif engine == "v":
+                nc.vector.tensor_copy(out=dst, in_=src)
+            else:
+                nc.scalar.activation(out=dst, in_=src, func=ACT.Copy)
+
+        def quantise_w(a, t0, t1):
+            cols = slice(P * t0, P * t1)
+            quantise(w_codes[a][:, cols], w_scales[a][:, cols], w_bf[a][:, t0:t1, :, :].rearrange("p t m j -> p (t m j)"))
+
+        x_words = keep.tile([P, S, 2], U32, name="x_words", align_bytes=64)
+
+        def gather(u):
+            nc.vector.tensor_copy(x_words[:, :, u], window[u][:].indirect(offsets[:]))
+
+        cast_x("v", 0, 0, 0, 512)
+        cast_x("v", 0, 1, 0, 320)
+        cast_x("s", 0, 1, 320, 512)
+        gather(0)
+        cast_x("s", 1, 0, 0, 512)
+        cast_x("v", 1, 1, 0, 320)
+        cast_x("s", 1, 1, 320, 512)
+        gather(1)
+        x_codes = keep.tile([P, S], U32, name="x_codes", align_bytes=64)
+        x_scales = keep.tile([P, S], U8, name="x_scales", align_bytes=64)
+        cast_w("s", 0, 0, 0, 64)
+
+        def quantise_x(d):
+            cols = slice(V * d, V * d + V)
+            quantise(x_codes[:, cols], x_scales[:, cols], x_words[:, cols, :].rearrange("p n u -> p (n u)").bitcast(BF16))
+
+        cast_w("v", 0, 1, 0, 32)
+        cast_w("s", 0, 1, 32, 64)
+        quantise_x(1)
+        quantise_w(0, 0, 2)
+        quantise_w(0, 2, 4)
+        quantise_x(0)
+
+        h_ps = {}
+        for c in range(2):
+            for d in (1, 0):
+                h_ps[d, c] = psum.tile([P, 4, P], F32, name=f"h_ps{d}{c}")
+                cols = slice(V * d + P * c, V * d + P * c + P)
+                for t in range(4):
+                    nc.tensor.matmul_mx(
+                        out=h_ps[d, c][:, t, :],
+                        lhsT=w_codes[0][:, P * t : P * t + P].bitcast(FP8X4),
+                        lhsT_scale=w_scales[0][:, P * t : P * t + P],
+                        rhs=x_codes[:, cols].bitcast(FP8X4),
+                        rhs_scale=x_scales[:, cols],
+                        start=True,
+                        stop=True,
+                    )
+        second = [keep.tile([P, P, 4], F32, name=f"second{c}") for c in range(2)]
+
+        def relu_second(c):
+            nc.scalar.activation(out=second[c][:], in_=h_ps[1, c][:].rearrange("p t n -> p n t"), func=ACT.Relu)
+
+        cast_w("s", 1, 0, 0, 64)
+        cast_w("v", 1, 1, 0, 40)
+        cast_w("s", 1, 1, 40, 64)
+        quantise_w(1, 0, 4)
+        relu_second(0)
+        cast_w("v", 2, 0, 0, 16)
+        cast_w("s", 2, 0, 16, 36)
+        relu_second(1)
+        cast_w("s", 2, 0, 36, 64)
+        cast_w("s", 2, 1, 0, 64)
+        band_codes = [keep.tile([P, V], U32, name=f"band_codes{b}", align_bytes=64) for b in range(2)]
+        band_scales = [keep.tile([P, V], U8, name=f"band_scales{b}", align_bytes=64) for b in range(2)]
+        band_bf = {}
+
+        def band(b, c):
+            band_bf[b, c] = keep.tile([P, P, 4], BF16, name=f"band_bf{b}{c}", align_bytes=64)
+            nc.vector.scalar_tensor_tensor(
+                out=band_bf[b, c][:],
+                in0=h_ps[0, c][:].rearrange("p t n -> p n t"),
+                scalar=0.0,
+                in1=second[c][:],
+                op0=ALU.max,
+                op1=(ALU.add, ALU.subtract)[b],
+            )
+
+        def quantise_band(b, c):
+            cols = slice(P * c, P * c + P)
+            quantise(band_codes[b][:, cols], band_scales[b][:, cols], band_bf[b, c][:].rearrange("p n t -> p (n t)"))
+
+        band(0, 0)
+        band(1, 0)
+        quantise_band(0, 0)
+        band(0, 1)
+        quantise_band(1, 0)
+        quantise_band(0, 1)
+        band(1, 1)
+        quantise_band(1, 1)
+
+        y_ps = [psum.tile([P, V], F32, name=f"y_ps{t}") for t in range(4)]
+
+        def second_product(b, t):
+            nc.tensor.matmul_mx(
+                out=y_ps[t][:],
+                lhsT=w_codes[1 + b][:, P * t : P * t + P].bitcast(FP8X4),
+                lhsT_scale=w_scales[1 + b][:, P * t : P * t + P],
+                rhs=band_codes[b][:].bitcast(FP8X4),
+                rhs_scale=band_scales[b][:],
+                start=(b == 0),
+                stop=(b == 1),
+            )
+
+        for t in range(4):
+            second_product(0, t)
+        y = keep.tile([P, 4, V], F32, name="y")
+        y_rows = out_0.rearrange("(p t) v -> p t v", t=4)
+        for t in range(4):
+            quantise_w(2, t, t + 1)
+            second_product(1, t)
+            nc.scalar.activation(out=y[:, t, :], in_=y_ps[t][:], func=ACT.Copy)
+            if t % 2 == 1:
+                nc.sync.dma_start(out=y_rows[:, t - 1 : t + 1, :], in_=y[:, t - 1 : t + 1, :])
+
+        y_words = keep.tile([P, V], I32, name="y_words", align_bytes=64)
+        y_scales = keep.tile([P, V], U8, name="y_scales", align_bytes=64)
+        y_bf = [keep.tile([P, P, 4], BF16, name=f"y_bf{c}", align_bytes=64) for c in range(2)]
+        for c in range(2):
+            nc.vector.tensor_copy(
+                out=y_bf[c][:].rearrange("p (n i) t -> p n t i", i=4),
+                in_=y[:, :, P * c : P * c + P].rearrange("p t (n i) -> p n t i", i=4),
+            )
+        for c in range(2):
+            cols = slice(P * c, P * c + P)
+            quantise(y_words[:, cols], y_scales[:, cols], y_bf[c][:].rearrange("p n t -> p (n t)"))
+        nc.sync.dma_start(out=out_1.rearrange("z p c r -> p (z c r)").bitcast(I32), in_=y_words[:])
+        scale_rows = out_2.rearrange("z q c -> (z q) c").bitcast(I32)
+        for q in range(4):
+            queue = nc.scalar if q % 2 == 0 else nc.sync
+            queue.dma_start(out=scale_rows[4 * q : 4 * q + 4, :], in_=y_scales[32 * q : 32 * q + 4, :].bitcast(I32))

@@ -49,18 +49,18 @@ def tile_picked_haar_relu_lo_kernel(tc, xT, w1, w2, w3, offs, out_0, out_1, out_
             src = x_raw[u, h][:, :, c0:c1].rearrange("p e c -> p c e")
             if engine == "v":
                 nc.vector.tensor_copy(out=dst, in_=src)
+            elif engine == "g":
+                nc.gpsimd.tensor_copy(out=dst, in_=src)
             else:
                 nc.scalar.activation(out=dst, in_=src, func=ACT.Copy)
 
-        w_bf = [keep.tile([P, 4, P, 4], BF16, name=f"w_bf{a}", align_bytes=64) for a in range(3)]
+        w_bf = {(a, r): keep.tile([P, 2, P, 4], BF16, name=f"w_bf{a}{r}", align_bytes=64) for a in range(3) for r in range(2)}
         w_codes = [keep.tile([P, H], U32, name=f"w_codes{a}", align_bytes=64) for a in range(3)]
         w_scales = [keep.tile([P, H], U8, name=f"w_scales{a}", align_bytes=64) for a in range(3)]
 
-        def cast_w(engine, a, h, m0, m1):
-            if m1 <= m0:
-                return
-            dst = w_bf[a][:, :, 64 * h + m0 : 64 * h + m1, :].rearrange("p t m j -> p m j t")
-            src = w_raw[a, h][:, :, 4 * m0 : 4 * m1].rearrange("p j (m t) -> p m j t", t=4)
+        def cast_w(engine, a, h, r):
+            dst = w_bf[a, r][:, :, 64 * h : 64 * h + 64, :].rearrange("p t m j -> p m j t")
+            src = w_raw[a, h][:].rearrange("p j (m t) -> p m j t", t=4)[:, :, :, 2 * r : 2 * r + 2]
             if a == 0:
                 if engine == "v":
                     nc.vector.tensor_scalar(out=dst, in0=src, scalar1=0.5, scalar2=None, op0=ALU.mult)
@@ -68,79 +68,54 @@ def tile_picked_haar_relu_lo_kernel(tc, xT, w1, w2, w3, offs, out_0, out_1, out_
                     nc.scalar.activation(out=dst, in_=src, func=ACT.Copy, scale=0.5)
             elif engine == "v":
                 nc.vector.tensor_copy(out=dst, in_=src)
+            elif engine == "g":
+                nc.gpsimd.tensor_copy(out=dst, in_=src)
             else:
                 nc.scalar.activation(out=dst, in_=src, func=ACT.Copy)
 
         def quantise_w(a, t0, t1):
             cols = slice(P * t0, P * t1)
-            quantise(w_codes[a][:, cols], w_scales[a][:, cols], w_bf[a][:, t0:t1, :, :].rearrange("p t m j -> p (t m j)"))
+            values = w_bf[a, t0 // 2][:, t0 % 2 : t0 % 2 + t1 - t0, :, :].rearrange("p t m j -> p (t m j)")
+            quantise(w_codes[a][:, cols], w_scales[a][:, cols], values)
 
-        x_words = keep.tile([P, S, 2], U32, name="x_words", align_bytes=64)
-
-        def gather(u):
-            nc.vector.tensor_copy(x_words[:, :, u], window[u][:].indirect(offsets[:]))
-
-        cast_x("v", 0, 0, 0, 512)
-        cast_x("v", 0, 1, 0, 320)
-        cast_x("s", 0, 1, 320, 512)
-        gather(0)
-        cast_x("s", 1, 0, 0, 512)
-        cast_x("v", 1, 1, 0, 320)
-        cast_x("s", 1, 1, 320, 512)
-        gather(1)
         x_codes = keep.tile([P, S], U32, name="x_codes", align_bytes=64)
         x_scales = keep.tile([P, S], U8, name="x_scales", align_bytes=64)
-        cast_w("s", 0, 0, 0, 64)
+        x_words = keep.tile([P, S, 2], U32, name="x_words", align_bytes=64)
 
-        def quantise_x(d):
-            cols = slice(V * d, V * d + V)
-            quantise(x_codes[:, cols], x_scales[:, cols], x_words[:, cols, :].rearrange("p n u -> p (n u)").bitcast(BF16))
+        def gather(u, n0, n1):
+            nc.vector.tensor_copy(x_words[:, n0:n1, u], window[u][:].indirect(offsets[:, n0 // 16 : n1 // 16]))
 
-        cast_w("v", 0, 1, 0, 32)
-        cast_w("s", 0, 1, 32, 64)
-        quantise_x(1)
-        quantise_w(0, 0, 2)
-        quantise_w(0, 2, 4)
-        quantise_x(0)
+        def quantise_x(n0, n1):
+            quantise(x_codes[:, n0:n1], x_scales[:, n0:n1], x_words[:, n0:n1, :].rearrange("p n u -> p (n u)").bitcast(BF16))
 
         h_ps = {}
-        for c in range(2):
-            for d in (1, 0):
-                h_ps[d, c] = psum.tile([P, 4, P], F32, name=f"h_ps{d}{c}")
-                cols = slice(V * d + P * c, V * d + P * c + P)
-                for t in range(4):
-                    nc.tensor.matmul_mx(
-                        out=h_ps[d, c][:, t, :],
-                        lhsT=w_codes[0][:, P * t : P * t + P].bitcast(FP8X4),
-                        lhsT_scale=w_scales[0][:, P * t : P * t + P],
-                        rhs=x_codes[:, cols].bitcast(FP8X4),
-                        rhs_scale=x_scales[:, cols],
-                        start=True,
-                        stop=True,
-                    )
+
+        def first_product(d, c):
+            h_ps[d, c] = psum.tile([P, 4, P], F32, name=f"h_ps{d}{c}", tag=f"bank{d}{c}")
+            cols = slice(V * d + P * c, V * d + P * c + P)
+            for t in range(4):
+                nc.tensor.matmul_mx(
+                    out=h_ps[d, c][:, t, :],
+                    lhsT=w_codes[0][:, P * t : P * t + P].bitcast(FP8X4),
+                    lhsT_scale=w_scales[0][:, P * t : P * t + P],
+                    rhs=x_codes[:, cols].bitcast(FP8X4),
+                    rhs_scale=x_scales[:, cols],
+                    start=True,
+                    stop=True,
+                )
+
         second = [keep.tile([P, P, 4], F32, name=f"second{c}") for c in range(2)]
 
         def relu_second(c):
             nc.scalar.activation(out=second[c][:], in_=h_ps[1, c][:].rearrange("p t n -> p n t"), func=ACT.Relu)
 
-        cast_w("s", 1, 0, 0, 64)
-        cast_w("v", 1, 1, 0, 40)
-        cast_w("s", 1, 1, 40, 64)
-        quantise_w(1, 0, 4)
-        relu_second(0)
-        cast_w("v", 2, 0, 0, 16)
-        cast_w("s", 2, 0, 16, 36)
-        relu_second(1)
-        cast_w("s", 2, 0, 36, 64)
-        cast_w("s", 2, 1, 0, 64)
-        band_codes = [keep.tile([P, V], U32, name=f"band_codes{b}", align_bytes=64) for b in range(2)]
-        band_scales = [keep.tile([P, V], U8, name=f"band_scales{b}", align_bytes=64) for b in range(2)]
-        band_bf = {}
+        band_codes = [keep.tile([P, 2, P], U32, name=f"band_codes{c}", align_bytes=64) for c in range(2)]
+        band_scales = [keep.tile([P, 2, P], U8, name=f"band_scales{c}", align_bytes=64) for c in range(2)]
+        band_bf = [keep.tile([P, 2, P, 4], BF16, name=f"band_bf{c}", align_bytes=64) for c in range(2)]
 
         def band(b, c):
-            band_bf[b, c] = keep.tile([P, P, 4], BF16, name=f"band_bf{b}{c}", align_bytes=64)
             nc.vector.scalar_tensor_tensor(
-                out=band_bf[b, c][:],
+                out=band_bf[c][:, b, :, :],
                 in0=h_ps[0, c][:].rearrange("p t n -> p n t"),
                 scalar=0.0,
                 in1=second[c][:],
@@ -148,55 +123,122 @@ def tile_picked_haar_relu_lo_kernel(tc, xT, w1, w2, w3, offs, out_0, out_1, out_
                 op1=(ALU.add, ALU.subtract)[b],
             )
 
-        def quantise_band(b, c):
-            cols = slice(P * c, P * c + P)
-            quantise(band_codes[b][:, cols], band_scales[b][:, cols], band_bf[b, c][:].rearrange("p n t -> p (n t)"))
+        def quantise_band(b0, b1, c):
+            quantise(
+                band_codes[c][:, b0:b1, :].rearrange("p b n -> p (b n)"),
+                band_scales[c][:, b0:b1, :].rearrange("p b n -> p (b n)"),
+                band_bf[c][:, b0:b1, :, :].rearrange("p b n t -> p (b n t)"),
+            )
 
-        band(0, 0)
-        band(1, 0)
-        quantise_band(0, 0)
-        band(0, 1)
-        quantise_band(1, 0)
-        quantise_band(0, 1)
-        band(1, 1)
-        quantise_band(1, 1)
+        y_ps = {}
 
-        y_ps = [psum.tile([P, V], F32, name=f"y_ps{t}") for t in range(4)]
-
-        def second_product(b, t):
+        def second_product(b, t, c):
+            if b == 0:
+                tag = f"out{t}" if c == 0 else ("bank10", "bank11", "bank00", "bank01")[t]
+                y_ps[t, c] = psum.tile([P, P], F32, name=f"y_ps{t}{c}", tag=tag)
             nc.tensor.matmul_mx(
-                out=y_ps[t][:],
+                out=y_ps[t, c][:],
                 lhsT=w_codes[1 + b][:, P * t : P * t + P].bitcast(FP8X4),
                 lhsT_scale=w_scales[1 + b][:, P * t : P * t + P],
-                rhs=band_codes[b][:].bitcast(FP8X4),
-                rhs_scale=band_scales[b][:],
+                rhs=band_codes[c][:, b, :].bitcast(FP8X4),
+                rhs_scale=band_scales[c][:, b, :],
                 start=(b == 0),
                 stop=(b == 1),
             )
 
-        for t in range(4):
-            second_product(0, t)
-        y = keep.tile([P, 4, V], F32, name="y")
-        y_rows = out_0.rearrange("(p t) v -> p t v", t=4)
-        for t in range(4):
-            quantise_w(2, t, t + 1)
-            second_product(1, t)
-            nc.scalar.activation(out=y[:, t, :], in_=y_ps[t][:], func=ACT.Copy)
-            if t % 2 == 1:
-                nc.sync.dma_start(out=y_rows[:, t - 1 : t + 1, :], in_=y[:, t - 1 : t + 1, :])
+        def second_products(b, c):
+            for t in range(4):
+                second_product(b, t, c)
 
+        y = [keep.tile([P, 4, P], F32, name=f"y{c}") for c in range(2)]
+        y_rows = out_0.rearrange("(p t) v -> p t v", t=4)
+        word_rows = out_1.rearrange("z p c r -> p (z c r)").bitcast(I32)
         y_words = keep.tile([P, V], I32, name="y_words", align_bytes=64)
         y_scales = keep.tile([P, V], U8, name="y_scales", align_bytes=64)
         y_bf = [keep.tile([P, P, 4], BF16, name=f"y_bf{c}", align_bytes=64) for c in range(2)]
-        for c in range(2):
+
+        def empty_y(engine, t, c):
+            if engine == "v":
+                nc.vector.tensor_copy(out=y[c][:, t, :], in_=y_ps[t, c][:])
+            else:
+                nc.scalar.activation(out=y[c][:, t, :], in_=y_ps[t, c][:], func=ACT.Copy)
+
+        def store_y(c):
+            nc.sync.dma_start(out=y_rows[:, :, P * c : P * c + P], in_=y[c][:])
+
+        def round_y(c):
             nc.vector.tensor_copy(
                 out=y_bf[c][:].rearrange("p (n i) t -> p n t i", i=4),
-                in_=y[:, :, P * c : P * c + P].rearrange("p t (n i) -> p n t i", i=4),
+                in_=y[c][:].rearrange("p t (n i) -> p n t i", i=4),
             )
-        for c in range(2):
+
+        def quantise_y(c):
             cols = slice(P * c, P * c + P)
             quantise(y_words[:, cols], y_scales[:, cols], y_bf[c][:].rearrange("p n t -> p (n t)"))
-        nc.sync.dma_start(out=out_1.rearrange("z p c r -> p (z c r)").bitcast(I32), in_=y_words[:])
+            nc.sync.dma_start(out=word_rows[:, cols], in_=y_words[:, cols])
+
+        cast_x("v", 0, 0, 0, 512)
+        cast_x("v", 0, 1, 0, 320)
+        cast_x("s", 0, 1, 320, 512)
+        gather(0, 0, 512)
+        cast_x("s", 1, 0, 0, 512)
+        cast_x("v", 1, 1, 0, 320)
+        cast_x("s", 1, 1, 320, 512)
+        gather(1, 256, 512)
+        gather(1, 0, 256)
+        cast_w("s", 0, 0, 0)
+        cast_w("s", 0, 0, 1)
+        quantise_x(256, 512)
+        cast_w("v", 0, 1, 0)
+        cast_w("s", 0, 1, 1)
+        quantise_w(0, 0, 2)
+        quantise_w(0, 2, 4)
+        quantise_x(0, 128)
+        quantise_x(128, 256)
+        first_product(1, 0)
+        first_product(0, 0)
+        first_product(1, 1)
+        first_product(0, 1)
+        cast_w("s", 1, 0, 0)
+        cast_w("s", 1, 0, 1)
+        relu_second(0)
+        relu_second(1)
+        cast_w("v", 1, 1, 0)
+        cast_w("v", 1, 1, 1)
+        band(0, 0)
+        band(1, 0)
+        quantise_w(1, 0, 2)
+        quantise_w(1, 2, 4)
+        band(0, 1)
+        quantise_band(0, 2, 0)
+        second_products(0, 0)
+        cast_w("s", 2, 0, 0)
+        cast_w("s", 2, 0, 1)
+        cast_w("s", 2, 1, 0)
+        cast_w("s", 2, 1, 1)
+        quantise_band(0, 1, 1)
+        band(1, 1)
+        second_products(0, 1)
+        quantise_w(2, 0, 2)
+        quantise_band(1, 2, 1)
+        quantise_w(2, 2, 4)
+        second_products(1, 0)
+        second_products(1, 1)
+        empty_y("s", 0, 0)
+        empty_y("s", 1, 0)
+        empty_y("v", 2, 0)
+        empty_y("s", 3, 0)
+        store_y(0)
+        empty_y("s", 0, 1)
+        round_y(0)
+        empty_y("s", 1, 1)
+        empty_y("s", 2, 1)
+        quantise_y(0)
+        empty_y("v", 3, 1)
+        store_y(1)
+        round_y(1)
+        quantise_y(1)
+
         scale_rows = out_2.rearrange("z q c -> (z q) c").bitcast(I32)
         for q in range(4):
             queue = nc.scalar if q % 2 == 0 else nc.sync

@@ -39,7 +39,7 @@ def tile_picked_haar_relu_lo_kernel(tc, xT, w1, w2, w3, offs, out_0, out_1, out_
         for a, w in enumerate((w1, w2, w3)):
             w_rows = w.rearrange("(p j) c -> p j c", j=4)
             for h in range(2):
-                w_raw[a, h] = keep.tile([P, 4, 256], F32, name=f"w_raw{a}{h}")
+                w_raw[a, h] = keep.tile([P, 4, 256], F32, name=f"w_raw{a}{h}", align_bytes=64)
                 nc.sync.dma_start(out=w_raw[a, h][:], in_=w_rows[:, :, 256 * h : 256 * h + 256])
 
         window = [keep.tile([P, T], U32, name=f"window{u}") for u in range(2)]
@@ -78,15 +78,17 @@ def tile_picked_haar_relu_lo_kernel(tc, xT, w1, w2, w3, offs, out_0, out_1, out_
             values = w_bf[a, t0 // 2][:, t0 % 2 : t0 % 2 + t1 - t0, :, :].rearrange("p t m j -> p (t m j)")
             quantise(w_codes[a][:, cols], w_scales[a][:, cols], values)
 
-        x_codes = keep.tile([P, S], U32, name="x_codes", align_bytes=64)
+        x_codes = {}
         x_scales = keep.tile([P, S], U8, name="x_scales", align_bytes=64)
         x_words = keep.tile([P, S, 2], U32, name="x_words", align_bytes=64)
 
         def gather(u, n0, n1):
             nc.vector.tensor_copy(x_words[:, n0:n1, u], window[u][:].indirect(offsets[:, n0 // 16 : n1 // 16]))
 
-        def quantise_x(n0, n1):
-            quantise(x_codes[:, n0:n1], x_scales[:, n0:n1], x_words[:, n0:n1, :].rearrange("p n u -> p (n u)").bitcast(BF16))
+        def quantise_x(d, c, tag):
+            x_codes[d, c] = keep.tile([P, P], U32, name=f"x_codes{d}{c}", tag=tag, align_bytes=64)
+            cols = slice(V * d + P * c, V * d + P * c + P)
+            quantise(x_codes[d, c][:], x_scales[:, cols], x_words[:, cols, :].rearrange("p n u -> p (n u)").bitcast(BF16))
 
         h_ps = {}
 
@@ -98,7 +100,7 @@ def tile_picked_haar_relu_lo_kernel(tc, xT, w1, w2, w3, offs, out_0, out_1, out_
                     out=h_ps[d, c][:, t, :],
                     lhsT=w_codes[0][:, P * t : P * t + P].bitcast(FP8X4),
                     lhsT_scale=w_scales[0][:, P * t : P * t + P],
-                    rhs=x_codes[:, cols].bitcast(FP8X4),
+                    rhs=x_codes[d, c][:].bitcast(FP8X4),
                     rhs_scale=x_scales[:, cols],
                     start=True,
                     stop=True,
@@ -184,33 +186,34 @@ def tile_picked_haar_relu_lo_kernel(tc, xT, w1, w2, w3, offs, out_0, out_1, out_
         cast_x("s", 1, 0, 0, 512)
         cast_x("v", 1, 1, 0, 320)
         cast_x("s", 1, 1, 320, 512)
-        gather(1, 256, 512)
-        gather(1, 0, 256)
+        gather(1, 0, 512)
         cast_w("s", 0, 0, 0)
         cast_w("s", 0, 0, 1)
-        quantise_x(256, 512)
+        quantise_x(1, 0, "x_codes10")
         cast_w("v", 0, 1, 0)
         cast_w("s", 0, 1, 1)
         quantise_w(0, 0, 2)
-        quantise_w(0, 2, 4)
-        quantise_x(0, 128)
-        quantise_x(128, 256)
+        quantise_w(0, 2, 3)
+        quantise_w(0, 3, 4)
         first_product(1, 0)
+        quantise_x(0, 0, "w_bf00")
         first_product(0, 0)
+        quantise_x(1, 1, "w_bf01")
         first_product(1, 1)
+        quantise_x(0, 1, "w_raw01")
         first_product(0, 1)
         cast_w("s", 1, 0, 0)
-        cast_w("s", 1, 0, 1)
         relu_second(0)
-        relu_second(1)
-        cast_w("v", 1, 1, 0)
-        cast_w("v", 1, 1, 1)
+        cast_w("v", 1, 0, 1)
         band(0, 0)
         band(1, 0)
-        quantise_w(1, 0, 2)
-        quantise_w(1, 2, 4)
+        cast_w("s", 1, 1, 0)
+        relu_second(1)
+        cast_w("v", 1, 1, 1)
         band(0, 1)
         quantise_band(0, 2, 0)
+        quantise_w(1, 0, 2)
+        quantise_w(1, 2, 4)
         second_products(0, 0)
         cast_w("s", 2, 0, 0)
         cast_w("s", 2, 0, 1)
@@ -220,9 +223,9 @@ def tile_picked_haar_relu_lo_kernel(tc, xT, w1, w2, w3, offs, out_0, out_1, out_
         band(1, 1)
         second_products(0, 1)
         quantise_w(2, 0, 2)
-        quantise_band(1, 2, 1)
         quantise_w(2, 2, 4)
         second_products(1, 0)
+        quantise_band(1, 2, 1)
         second_products(1, 1)
         empty_y("s", 0, 0)
         empty_y("s", 1, 0)

@@ -152,7 +152,7 @@ def tile_picked_haar_relu_lo_kernel(tc, xT, w1, w2, w3, offs, out_0, out_1, out_
             for t in range(4):
                 second_product(b, t, c)
 
-        y = [keep.tile([P, 4, P], F32, name=f"y{c}") for c in range(2)]
+        y = keep.tile([P, 4, V], F32, name="y")
         y_rows = out_0.rearrange("(p t) v -> p t v", t=4)
         word_rows = out_1.rearrange("z p c r -> p (z c r)").bitcast(I32)
         y_words = keep.tile([P, V], I32, name="y_words", align_bytes=64)
@@ -161,23 +161,24 @@ def tile_picked_haar_relu_lo_kernel(tc, xT, w1, w2, w3, offs, out_0, out_1, out_
 
         def empty_y(engine, t, c):
             if engine == "v":
-                nc.vector.tensor_copy(out=y[c][:, t, :], in_=y_ps[t, c][:])
+                nc.vector.tensor_copy(out=y[:, t, P * c : P * c + P], in_=y_ps[t, c][:])
             else:
-                nc.scalar.activation(out=y[c][:, t, :], in_=y_ps[t, c][:], func=ACT.Copy)
+                nc.scalar.activation(out=y[:, t, P * c : P * c + P], in_=y_ps[t, c][:], func=ACT.Copy)
 
-        def store_y(c):
-            nc.sync.dma_start(out=y_rows[:, :, P * c : P * c + P], in_=y[c][:])
+        def store_y(t0, t1):
+            nc.sync.dma_start(out=y_rows[:, t0:t1, :], in_=y[:, t0:t1, :])
 
-        def round_y(c):
-            nc.vector.tensor_copy(
-                out=y_bf[c][:].rearrange("p (n i) t -> p n t i", i=4),
-                in_=y[c][:].rearrange("p t (n i) -> p n t i", i=4),
-            )
+        def round_y(engine, c):
+            dst = y_bf[c][:].rearrange("p (n i) t -> p n t i", i=4)
+            src = y[:, :, P * c : P * c + P].rearrange("p t (n i) -> p n t i", i=4)
+            if engine == "v":
+                nc.vector.tensor_copy(out=dst, in_=src)
+            else:
+                nc.scalar.activation(out=dst, in_=src, func=ACT.Copy)
 
         def quantise_y(c):
             cols = slice(P * c, P * c + P)
             quantise(y_words[:, cols], y_scales[:, cols], y_bf[c][:].rearrange("p n t -> p (n t)"))
-            nc.sync.dma_start(out=word_rows[:, cols], in_=y_words[:, cols])
 
         cast_x("v", 0, 0, 0, 512)
         cast_x("v", 0, 1, 0, 320)
@@ -223,25 +224,21 @@ def tile_picked_haar_relu_lo_kernel(tc, xT, w1, w2, w3, offs, out_0, out_1, out_
         band(1, 1)
         second_products(0, 1)
         quantise_w(2, 0, 2)
-        quantise_w(2, 2, 4)
-        second_products(1, 0)
         quantise_band(1, 2, 1)
-        second_products(1, 1)
-        empty_y("s", 0, 0)
-        empty_y("s", 1, 0)
-        empty_y("v", 2, 0)
-        empty_y("s", 3, 0)
-        store_y(0)
-        empty_y("s", 0, 1)
-        round_y(0)
-        empty_y("s", 1, 1)
-        empty_y("s", 2, 1)
-        quantise_y(0)
-        empty_y("v", 3, 1)
-        store_y(1)
-        round_y(1)
+        quantise_w(2, 2, 3)
+        quantise_w(2, 3, 4)
+        for t in range(4):
+            for c in range(2):
+                second_product(1, t, c)
+                empty_y("s" if t < 2 or c == 0 else "v", t, c)
+            if t % 2 == 1:
+                store_y(t - 1, t + 1)
+        round_y("s", 0)
+        round_y("v", 1)
         quantise_y(1)
+        quantise_y(0)
 
+        nc.sync.dma_start(out=word_rows, in_=y_words[:])
         scale_rows = out_2.rearrange("z q c -> (z q) c").bitcast(I32)
         for q in range(4):
             queue = nc.scalar if q % 2 == 0 else nc.sync

from contextlib import ExitStack

import concourse.mybir as mybir

F32 = mybir.dt.float32
BF16 = mybir.dt.bfloat16
U32 = mybir.dt.uint32
I32 = mybir.dt.int32
U16 = mybir.dt.uint16
U8 = mybir.dt.uint8
FP8X4 = mybir.dt.float8_e4m3fn_x4
ALU = mybir.AluOpType
ACT = mybir.ActivationFunctionType

P = 128
K, T, S, V, H = 512, 1024, 512, 256, 512
FLOPS = 2 * K * H * S + 2 * 2 * H * H * V


def tile_picked_haar_relu_lo_kernel(tc, xT, w1, w2, w3, offs, out_0, out_1, out_2):
    nc = tc.nc
    with ExitStack() as ctx:
        keep = ctx.enter_context(tc.tile_pool(name="keep", bufs=1))
        psum = ctx.enter_context(tc.psum_pool(name="psum", bufs=1))

        def quantise(codes, scales, values):
            nc.vector.quantize_mx(out=codes.bitcast(FP8X4), scales=scales, in_=values)

        x_rows = xT.rearrange("(p j) c -> p j c", j=4)
        offsets = keep.tile([P, S // 16], U16, name="offsets")
        x_raw = {}
        for u in range(2):
            for h in range(2):
                x_raw[u, h] = keep.tile([P, 2, 512], F32, name=f"x_raw{u}{h}")
                nc.sync.dma_start(out=x_raw[u, h][:], in_=x_rows[:, 2 * u : 2 * u + 2, 512 * h : 512 * h + 512])
                if (u, h) == (0, 0):
                    nc.sync.dma_start(offsets[:], offs)
        w_raw = {}
        for a, w in enumerate((w1, w2, w3)):
            w_rows = w.rearrange("(p j) c -> p j c", j=4)
            for h in range(2):
                w_raw[a, h] = keep.tile([P, 4, 256], F32, name=f"w_raw{a}{h}", align_bytes=64)
                nc.sync.dma_start(out=w_raw[a, h][:], in_=w_rows[:, :, 256 * h : 256 * h + 256])

        window = [keep.tile([P, T], U32, name=f"window{u}") for u in range(2)]

        def cast_x(engine, u, h, c0, c1):
            dst = window[u][:].bitcast(BF16).rearrange("p (c e) -> p c e", e=2)[:, 512 * h + c0 : 512 * h + c1, :]
            src = x_raw[u, h][:, :, c0:c1].rearrange("p e c -> p c e")
            if engine == "v":
                nc.vector.tensor_copy(out=dst, in_=src)
            elif engine == "g":
                nc.gpsimd.tensor_copy(out=dst, in_=src)
            else:
                nc.scalar.activation(out=dst, in_=src, func=ACT.Copy)

        w_bf = {(a, r): keep.tile([P, 2, P, 4], BF16, name=f"w_bf{a}{r}", align_bytes=64) for a in range(3) for r in range(2)}
        w_codes = [keep.tile([P, H], U32, name=f"w_codes{a}", align_bytes=64) for a in range(3)]
        w_scales = [keep.tile([P, H], U8, name=f"w_scales{a}", align_bytes=64) for a in range(3)]

        def cast_w(engine, a, h, r):
            dst = w_bf[a, r][:, :, 64 * h : 64 * h + 64, :].rearrange("p t m j -> p m j t")
            src = w_raw[a, h][:].rearrange("p j (m t) -> p m j t", t=4)[:, :, :, 2 * r : 2 * r + 2]
            if a == 0:
                if engine == "v":
                    nc.vector.tensor_scalar(out=dst, in0=src, scalar1=0.5, scalar2=None, op0=ALU.mult)
                else:
                    nc.scalar.activation(out=dst, in_=src, func=ACT.Copy, scale=0.5)
            elif engine == "v":
                nc.vector.tensor_copy(out=dst, in_=src)
            elif engine == "g":
                nc.gpsimd.tensor_copy(out=dst, in_=src)
            else:
                nc.scalar.activation(out=dst, in_=src, func=ACT.Copy)

        def quantise_w(a, t0, t1):
            cols = slice(P * t0, P * t1)
            values = w_bf[a, t0 // 2][:, t0 % 2 : t0 % 2 + t1 - t0, :, :].rearrange("p t m j -> p (t m j)")
            quantise(w_codes[a][:, cols], w_scales[a][:, cols], values)

        x_codes = {}
        x_scales = keep.tile([P, S], U8, name="x_scales", align_bytes=64)
        x_words = keep.tile([P, S, 2], U32, name="x_words", align_bytes=64)

        def gather(u, n0, n1):
            nc.vector.tensor_copy(x_words[:, n0:n1, u], window[u][:].indirect(offsets[:, n0 // 16 : n1 // 16]))

        def quantise_x(d, c, tag):
            x_codes[d, c] = keep.tile([P, P], U32, name=f"x_codes{d}{c}", tag=tag, align_bytes=64)
            cols = slice(V * d + P * c, V * d + P * c + P)
            quantise(x_codes[d, c][:], x_scales[:, cols], x_words[:, cols, :].rearrange("p n u -> p (n u)").bitcast(BF16))

        h_ps = {}

        def first_product(d, c):
            h_ps[d, c] = psum.tile([P, 4, P], F32, name=f"h_ps{d}{c}", tag=f"bank{d}{c}")
            cols = slice(V * d + P * c, V * d + P * c + P)
            for t in range(4):
                nc.tensor.matmul_mx(
                    out=h_ps[d, c][:, t, :],
                    lhsT=w_codes[0][:, P * t : P * t + P].bitcast(FP8X4),
                    lhsT_scale=w_scales[0][:, P * t : P * t + P],
                    rhs=x_codes[d, c][:].bitcast(FP8X4),
                    rhs_scale=x_scales[:, cols],
                    start=True,
                    stop=True,
                )

        second = [keep.tile([P, P, 4], F32, name=f"second{c}") for c in range(2)]

        def relu_second(c):
            nc.scalar.activation(out=second[c][:], in_=h_ps[1, c][:].rearrange("p t n -> p n t"), func=ACT.Relu)

        band_codes = [keep.tile([P, 2, P], U32, name=f"band_codes{c}", align_bytes=64) for c in range(2)]
        band_scales = [keep.tile([P, 2, P], U8, name=f"band_scales{c}", align_bytes=64) for c in range(2)]
        band_bf = [keep.tile([P, 2, P, 4], BF16, name=f"band_bf{c}", align_bytes=64) for c in range(2)]

        def band(b, c):
            nc.vector.scalar_tensor_tensor(
                out=band_bf[c][:, b, :, :],
                in0=h_ps[0, c][:].rearrange("p t n -> p n t"),
                scalar=0.0,
                in1=second[c][:],
                op0=ALU.max,
                op1=(ALU.add, ALU.subtract)[b],
            )

        def quantise_band(b0, b1, c):
            quantise(
                band_codes[c][:, b0:b1, :].rearrange("p b n -> p (b n)"),
                band_scales[c][:, b0:b1, :].rearrange("p b n -> p (b n)"),
                band_bf[c][:, b0:b1, :, :].rearrange("p b n t -> p (b n t)"),
            )

        y_ps = {}

        def second_product(b, t, c):
            if b == 0:
                tag = f"out{t}" if c == 0 else ("bank10", "bank11", "bank00", "bank01")[t]
                y_ps[t, c] = psum.tile([P, P], F32, name=f"y_ps{t}{c}", tag=tag)
            nc.tensor.matmul_mx(
                out=y_ps[t, c][:],
                lhsT=w_codes[1 + b][:, P * t : P * t + P].bitcast(FP8X4),
                lhsT_scale=w_scales[1 + b][:, P * t : P * t + P],
                rhs=band_codes[c][:, b, :].bitcast(FP8X4),
                rhs_scale=band_scales[c][:, b, :],
                start=(b == 0),
                stop=(b == 1),
            )

        def second_products(b, c):
            for t in range(4):
                second_product(b, t, c)

        y = keep.tile([P, 4, V], F32, name="y")
        y_rows = out_0.rearrange("(p t) v -> p t v", t=4)
        word_rows = out_1.rearrange("z p c r -> p (z c r)").bitcast(I32)
        y_words = keep.tile([P, V], I32, name="y_words", align_bytes=64)
        y_scales = keep.tile([P, V], U8, name="y_scales", align_bytes=64)
        y_bf = [keep.tile([P, P, 4], BF16, name=f"y_bf{c}", align_bytes=64) for c in range(2)]

        def empty_y(engine, t, c):
            if engine == "v":
                nc.vector.tensor_copy(out=y[:, t, P * c : P * c + P], in_=y_ps[t, c][:])
            else:
                nc.scalar.activation(out=y[:, t, P * c : P * c + P], in_=y_ps[t, c][:], func=ACT.Copy)

        def store_y(t0, t1):
            nc.sync.dma_start(out=y_rows[:, t0:t1, :], in_=y[:, t0:t1, :])

        def round_y(engine, c):
            dst = y_bf[c][:].rearrange("p (n i) t -> p n t i", i=4)
            src = y[:, :, P * c : P * c + P].rearrange("p t (n i) -> p n t i", i=4)
            if engine == "v":
                nc.vector.tensor_copy(out=dst, in_=src)
            else:
                nc.scalar.activation(out=dst, in_=src, func=ACT.Copy)

        def quantise_y(c):
            cols = slice(P * c, P * c + P)
            quantise(y_words[:, cols], y_scales[:, cols], y_bf[c][:].rearrange("p n t -> p (n t)"))

        cast_x("v", 0, 0, 0, 512)
        cast_x("v", 0, 1, 0, 320)
        cast_x("s", 0, 1, 320, 512)
        gather(0, 0, 512)
        cast_x("s", 1, 0, 0, 512)
        cast_x("v", 1, 1, 0, 320)
        cast_x("s", 1, 1, 320, 512)
        gather(1, 0, 512)
        cast_w("s", 0, 0, 0)
        cast_w("s", 0, 0, 1)
        quantise_x(1, 0, "x_codes10")
        cast_w("v", 0, 1, 0)
        cast_w("s", 0, 1, 1)
        quantise_w(0, 0, 2)
        quantise_w(0, 2, 3)
        quantise_w(0, 3, 4)
        first_product(1, 0)
        quantise_x(0, 0, "w_bf00")
        first_product(0, 0)
        quantise_x(1, 1, "w_bf01")
        first_product(1, 1)
        quantise_x(0, 1, "w_raw01")
        first_product(0, 1)
        cast_w("s", 1, 0, 0)
        relu_second(0)
        cast_w("v", 1, 0, 1)
        band(0, 0)
        band(1, 0)
        cast_w("s", 1, 1, 0)
        relu_second(1)
        cast_w("v", 1, 1, 1)
        band(0, 1)
        quantise_band(0, 2, 0)
        quantise_w(1, 0, 2)
        quantise_w(1, 2, 4)
        second_products(0, 0)
        cast_w("s", 2, 0, 0)
        cast_w("s", 2, 0, 1)
        cast_w("s", 2, 1, 0)
        cast_w("s", 2, 1, 1)
        quantise_band(0, 1, 1)
        band(1, 1)
        second_products(0, 1)
        quantise_w(2, 0, 2)
        quantise_band(1, 2, 1)
        quantise_w(2, 2, 3)
        quantise_w(2, 3, 4)
        for t in range(4):
            for c in range(2):
                second_product(1, t, c)
                empty_y("s" if t < 2 or c == 0 else "v", t, c)
            if t % 2 == 1:
                store_y(t - 1, t + 1)
        round_y("s", 0)
        round_y("v", 1)
        quantise_y(1)
        quantise_y(0)

        nc.sync.dma_start(out=word_rows, in_=y_words[:])
        scale_rows = out_2.rearrange("z q c -> (z q) c").bitcast(I32)
        for q in range(4):
            queue = nc.scalar if q % 2 == 0 else nc.sync
            queue.dma_start(out=scale_rows[4 * q : 4 * q + 4, :], in_=y_scales[32 * q : 32 * q + 4, :].bitcast(I32))
